import numpy as np, ml_dtypes
CORES = [8,9,10,11,12,13]
N = 6
BF = ml_dtypes.bfloat16
def gentries(a):
    return np.ascontiguousarray(a.reshape(8, 16, -1).transpose(0, 2, 1)).reshape(8, -1)
def gtable(e):
    e = np.asarray(e); return np.ascontiguousarray(e.reshape(8, -1, 16).transpose(0, 2, 1)).reshape(128, -1).astype(np.int32)
R, A, LV, Q = 2048, 2, 1, 64
def level(kids, h):
    return kids[h // LV].reshape(8, LV, R, A)[:, h % LV]
def sizes(kids, runs):
    s = [runs[0].astype(np.int64)]
    for h in range(N * LV):
        s.append(np.sum(s[-1][np.arange(8)[:, None, None], level(kids, h)], axis=-1))
    return s
def parts(kids, s, h, n):
    g = np.arange(8)[:, None]; c = level(kids, h)[g, n]
    e = np.add.accumulate(s[h][g[:, :, None], c], axis=-1)
    return c, np.concatenate([np.zeros_like(e[..., :1]), e[..., :-1]], axis=-1)
def put(d, tops, offs):
    d["top"] = np.stack([gtable(v) for v in tops]); d["off"] = np.stack([gtable(v) for v in offs]); return d
def ask(d, tops, u):
    z = sizes(d["kids"], d["runs"])[-1][np.arange(8)[None, :, None], tops]
    return put(d, tops, np.minimum((u * z).astype(np.int64), z - 1))
def setup_inputs(rng):
    d = {"kids": rng.integers(0, R, (N, 8, LV * A * R)).astype(np.int32), "letter": rng.integers(0, 1 << 24, (N, 8, R)).astype(np.int32), "runs": rng.integers(1, 16, (N, 8, R)).astype(np.int32)}
    return ask(d, rng.integers(0, R, (N, 8, Q)), rng.random((N, 8, Q)))
def setup_inputs_edges(rng):
    d = setup_inputs(rng); k = d["kids"]; d["kids"] = np.where(rng.random(k.shape) < 0.25, rng.choice(np.array([0, R - 1]), k.shape), k).astype(np.int32)
    s = sizes(d["kids"], d["runs"]); tops = rng.integers(0, R, (N, 8, Q)); tops[:, :, 0] = 0; tops[:, :, 1] = R - 1; offs = np.zeros((N, 8, Q), np.int64)
    for r in range(N):
        n = tops[r]; low = rng.integers(0, N * LV + 1, (8, Q)); last = rng.integers(0, 2, (8, Q))
        for h in range(N * LV - 1, -1, -1):
            b = np.where(h < low, last * (A - 1), rng.integers(0, A, (8, Q)))[..., None]
            c, w = parts(d["kids"], s, h, n)
            offs[r] += np.take_along_axis(w, b, -1)[..., 0]; n = np.take_along_axis(c, b, -1)[..., 0]
        offs[r] += last * (s[0][np.arange(8)[:, None], n] - 1)
    return put(d, tops, offs)
def setup_inputs_runs(rng):
    d = setup_inputs(rng); d["runs"] = rng.choice(np.array([1, 15]), (N, 8, R)).astype(np.int32); a, b = rng.permutation(8)[:2]
    d["runs"][0, a] = 15; d["runs"][0, b] = 1
    u = rng.random((N, 8, Q)); m = rng.integers(0, 4, u.shape); u = np.where(m == 0, 0.0, np.where(m == 1, 1.0, u))
    return ask(d, rng.integers(0, R, (N, 8, Q)), u)
def setup_inputs_one(rng):
    d = setup_inputs(rng); k = d["kids"].reshape(N, 8, LV * R, A); t = rng.random((N, 8, LV * R, 1)) < 0.5
    d["kids"] = np.where(t, k[..., :1], k).reshape(N, 8, LV * A * R).astype(np.int32)
    tops = np.repeat(rng.integers(0, R, (N, 8, 1)), Q, axis=2); z = sizes(d["kids"], d["runs"])[-1][np.arange(8)[None, :, None], tops]
    start = (rng.random((N, 8, 1)) * z[:, :, :1]).astype(np.int64)
    offs = (start + np.arange(Q)[None, None, :]) % z; q = rng.integers(0, N)
    offs[q] = np.minimum((rng.random((8, 1)) * z[q]).astype(np.int64), z[q] - 1)
    return put(d, tops, offs)
def setup_inputs_spread(rng):
    d = setup_inputs(rng)
    d["kids"] = np.minimum((R * rng.random((N, 8, LV * A * R)) ** 4).astype(np.int32), R - 1)
    d["letter"] = np.minimum(np.exp2(24 * rng.random((N, 8, R))).astype(np.int32), (1 << 24) - 1)
    d["runs"] = np.minimum(1 + (15 * rng.random((N, 8, R)) ** 3).astype(np.int32), 15).astype(np.int32)
    return ask(d, np.minimum((R * rng.random((N, 8, Q)) ** 3).astype(np.int64), R - 1), rng.random((N, 8, Q)) ** 2)
def check_inputs(d):
    bad = []
    for k, lo, hi in (("kids", 0, R - 1), ("letter", 0, (1 << 24) - 1), ("runs", 1, 15), ("top", 0, R - 1)):
        if d[k].min() < lo or d[k].max() > hi: bad.append(k)
    if bad: return bad
    z = sizes(d["kids"], d["runs"])[-1]
    for r in range(N):
        o = gentries(d["off"][r]); n = gentries(d["top"][r])
        if (o < 0).any() or (o >= z[np.arange(8)[:, None], n]).any(): return ["off"]
    return []
def reference(kids, letter, runs, top, off):
    s = sizes(kids, runs); y = np.zeros((N, 8, Q), np.float32)
    for r in range(N):
        n = gentries(top[r]).astype(np.int64); o = gentries(off[r]).astype(np.int64)
        for h in range(N * LV - 1, -1, -1):
            c, w = parts(kids, s, h, n)
            b = np.sum(o[..., None] >= w[..., 1:], axis=-1)[..., None]
            o = o - np.take_along_axis(w, b, -1)[..., 0]; n = np.take_along_axis(c, b, -1)[..., 0]
        y[r] = letter[0][np.arange(8)[:, None], n]
    return {"y": y}

from concourse.bass import DstId, RemoteDMATransfer
from concourse.mybir import AluOpType, ActivationFunctionType

F, I, U, B = "float32", "int32", "uint16", "bfloat16"
SCRATCH = {
    "raw": ("sbuf", [128, 256], I), "fa": ("sbuf", [128, 256], F), "fb": ("sbuf", [128, 256], F),
    "sl": ("sbuf", [128, 256], U), "rr": ("sbuf", [128, 128], I), "rl": ("sbuf", [128, 128], I),
    "rb": ("sbuf", [128, 128], B), "lf": ("sbuf", [128, 128], F),
    "tq": ("sbuf", [128, 64], I), "tf": ("sbuf", [128, 64], F), "tt": ("sbuf", [128, 64], F), "xq": ("sbuf", [128, 8], F),
    "pint": ("sbuf", [128, 1], I), "ci": ("sbuf", [128, 8], I), "cf": ("sbuf", [128, 8], F), "cc": ("sbuf", [128, 32], F),
    "pf": ("sbuf", [128, 1], F), "hcol": ("sbuf", [128, 8], F),
    "lkf": ("sbuf", [128, 16], F), "lk": ("sbuf", [128, 16], U), "elf": ("sbuf", [128, 12], F), "el": ("sbuf", [128, 12], U),
    "iw": ("sbuf", [128, 256], F), "rv": ("sbuf", [128, 128], F), "m1": ("sbuf", [128, 128], F), "m2": ("sbuf", [128, 128], F),
    "lm": ("sbuf", [128, 768], B), "sw": ("sbuf", [128, 512], F), "msk": ("sbuf", [128, 48], F),
    "w0": ("sbuf", [128, 2048], B), "w1": ("sbuf", [128, 2048], B), "w2": ("sbuf", [128, 2048], B),
    "w3": ("sbuf", [128, 2048], F), "wt": ("sbuf", [128, 2048], F), "gt": ("sbuf", [128, 1024], B),
    "ls0": ("sbuf", [128, 64], U), "ls1": ("sbuf", [128, 64], U), "ls2": ("sbuf", [128, 64], U),
    "ql": ("sbuf", [128, 12], F), "l5": ("sbuf", [128, 6], U), "l4": ("sbuf", [128, 16], U), "l3": ("sbuf", [128, 32], U),
    "lq": ("sbuf", [128, 48], U), "nf": ("sbuf", [128, 48], F), "nn": ("sbuf", [128, 48], F), "ndn": ("sbuf", [128, 48], F),
    "g5": ("sbuf", [128, 96], F), "d5": ("sbuf", [128, 128], F), "g4": ("sbuf", [128, 192], F), "d4": ("sbuf", [128, 256], F),
    "g3": ("sbuf", [128, 384], F), "d3": ("sbuf", [128, 384], F), "gq": ("sbuf", [128, 768], B), "dq": ("sbuf", [128, 768], B),
    "orep": ("sbuf", [128, 48], F), "base": ("sbuf", [128, 12], F), "cum": ("sbuf", [128, 48], F), "ge": ("sbuf", [128, 48], F),
    "pr": ("sbuf", [128, 96], F), "rs": ("sbuf", [128, 96], F), "fin": ("sbuf", [128, 12], F), "l2": ("sbuf", [128, 12], U),
    "g2": ("sbuf", [128, 192], F), "d2": ("sbuf", [128, 192], F), "hh": ("sbuf", [128, 96], F), "nm": ("sbuf", [128, 96], F),
    "hl": ("sbuf", [128, 96], F), "sel": ("sbuf", [128, 96], F), "l1": ("sbuf", [128, 6], U),
    "g1": ("sbuf", [128, 96], F), "d1": ("sbuf", [128, 96], F),
    "druns": ("dram", [128, 32], B), "dtop": ("dram", [7, 128, 32], F), "dans": ("dram", [4, 128, 1], F),
}
for _b in range(8):
    SCRATCH["ps%d" % _b] = ("psum", [128, 512], F)
POOL = 130
SEMAPHORES = ["aruns", "al0", "al1", "al2", "atop", "aq", "aans", "sent"] + ["p%d" % k for k in range(POOL)]
OWNERS = [2, 3, 4, 5]
A = AluOpType
COPY = ActivationFunctionType.Copy
IDENT = ActivationFunctionType.Identity


def shares(n, total):
    k = 1
    while 2 * k * n <= total:
        k *= 2
    out = [k] * n
    for i in range(n):
        if sum(out) + k <= total:
            out[i] = 2 * k
    return out


def even(n, total):
    k = min(shares(n, total))
    return [k] * n


def rank_program(g, core, T, topo):
    rank = T.rank_of(core)
    if rank is None:
        return
    cores = T.cores
    NE = len(topo.engines(cores[0], cores[1]))
    own = OWNERS.index(rank) if rank in OWNERS else None
    Q = {"v": g.vector, "s": g.scalar, "t": g.tensor, "g": g, "y": g.sync}
    V, S, PE = g.vector, g.scalar, g.tensor
    nxt = [0]
    total, seen, cur = {}, {}, {}

    def fresh():
        name = "p%d" % nxt[0]
        nxt[0] += 1
        total[name] = 0
        return name

    def emit(q, ins):
        if q not in cur:
            cur[q] = fresh()
        ins.then_inc(T.sem[cur[q]], 1)
        total[cur[q]] += 1

    def wait(q, *toks):
        for tk in toks:
            if tk is None or tk[1] == 0 or seen.get((q, tk[0]), 0) >= tk[1]:
                continue
            Q[q].wait_ge(T.sem[tk[0]], tk[1])
            seen[(q, tk[0])] = tk[1]

    def tok(q):
        name = cur.pop(q)
        return (name, total[name])

    def sync(q):
        if q in cur:
            wait(q, (cur[q], total[cur[q]]))

    def dma(q, name, out, in_):
        Q[q].dma_start(out, in_).then_inc(T.sem[name], 16)
        total[name] += 16

    def send(items, counts, sem):
        trs, at = [], 0
        for (r, src, dst), k in zip(items, counts):
            rid, pid, _ = topo.addr(cores[r])
            m = sum(1 << e for e in topo.engines(core, cores[r])[at:at + k])
            at += k
            trs.append(RemoteDMATransfer(dst_ids=[DstId(rid=rid, pnc=pid)], dma_engine_mask=m, remote_sem=T.sem[sem], src=src, dst=dst))
        g.remote_dma_fused(trs, local_sem=T.sem.sent)
        total["sent"] = total.get("sent", 0) + sum(counts)

    def ts(out, in0, s1, op0, s2=None, op1=None):
        if op1 is None:
            emit("v", V.tensor_scalar(out, in0, s1, None, op0))
        else:
            emit("v", V.tensor_scalar(out, in0, s1, s2, op0, op1))

    def tt(out, a, b, op):
        emit("v", V.tensor_tensor(out, a, b, op))

    def cp(q, out, in_):
        emit(q, V.tensor_copy(out, in_) if q == "v" else S.activation(out, in_, COPY))

    def dests(r):
        return [o for o in range(4) if OWNERS[o] != r]

    def ans_dests(o):
        return [r for r in range(6) if r != OWNERS[o]]

    two = ("y", "s")
    if rank == 0:
        s_r = fresh()
        for o in range(4):
            dma(two[o % 2], s_r, T.rr[:, 32 * o:32 * o + 32], T.runs[2 * o:2 * o + 2, :])
    s_k = fresh()
    for o in range(4):
        dma(two[o % 2], s_k, T.raw[:, 64 * o:64 * o + 64], T.kids[2 * o:2 * o + 2, :])
    if rank == 0:
        s_l = fresh()
        for o in range(4):
            dma(two[o % 2], s_l, T.rl[:, 32 * o:32 * o + 32], T.letter[2 * o:2 * o + 2, :])
    s_q = fresh()
    dma("y", s_q, T.tq[0:8, :], T.top[:, :])
    dma("s" if own is None else "y", s_q, T.tq[8:16, :], T.off[:, :])

    fl = dict(allow_small_or_imprecise_dtypes=True)
    k_g1 = k_g2 = None
    if rank < 3 or own is not None:
        emit("g", g.iota(T.pint[:], [[0, 1]], 0, 1))
        k_p = tok("g")
    if own is not None:
        emit("g", g.iota(T.iw[:], [[1, 256]], 0, 0, **fl))
        k_g1 = tok("g")
    if rank < 3:
        emit("g", g.iota(T.lkf[:], [[32, 2], [64, 4], [1, 2]], 0, 0, **fl))
        k_lk = tok("g")
    if own is not None:
        emit("g", g.iota(T.rv[:], [[16, 2], [0, 4], [1, 16]], 0, 0, **fl))
        emit("g", g.iota(T.elf[:, 0:2], [[0, 2]], 0, 0, **fl))
        emit("g", g.iota(T.elf[:, 2:4], [[128, 2]], 2, 0, **fl))
        emit("g", g.iota(T.elf[:, 4:8], [[128, 4]], 4, 0, **fl))
        k_g2 = tok("g")

    def c(k):
        return T.cc[:, k:k + 1]

    def d(k):
        return T.cf[:, k:k + 1]

    MLO, MHI, TWO, GB, AA, TAU, K1, MA0, NPAR, C1, PP, PM, ORC, T0, T1, U15, CPI, LO, HI1, HI = range(20)
    emit("v", V.memset(T.tf[0:32, :], 0.0))
    if rank < 3 or own is not None:
        wait("v", k_p)
        ts(T.ci[:, 0:1], T.pint[:], 15, A.bitwise_and)
        if own is not None:
            for k, (sh, m) in enumerate([(4, 1), (5, 1), (6, 1), (0, 3), (0, 12), (0, 1), (1, 1)]):
                ts(T.ci[:, k + 1:k + 2], T.pint[:], sh, A.logical_shift_right, m, A.bitwise_and)
            cp("v", T.pf[:], T.pint[:])
        sync("v")
        n = 8 if own is not None else 1
        cp("v", T.cf[:, 0:n], T.ci[:, 0:n])
        sync("v")
        if own is not None:
            ts(c(MLO), d(0), 8.0, A.is_equal)
            ts(c(MHI), d(0), 4.0, A.is_equal)
        if rank < 3:
            ts(c(TWO), d(0), 2.0, A.mult)
        sync("v")
        if own is not None:
            wait("v", k_g1)
            ts(T.hcol[:], T.iw[:, 0:8], c(MHI), A.mult, 256.0, A.mult)
        if rank < 3:
            wait("v", k_lk)
            ts(T.lk[:], T.lkf[:], c(TWO), A.add)
    k_c1 = tok("v")
    wait("v", k_c1)
    if own is not None:
        wait("s", k_c1, k_g1)
        for h in range(8):
            emit("s", S.activation(T.w0[:, 256 * h:256 * h + 256], T.iw[:], IDENT, bias=T.hcol[:, h:h + 1], scale=c(MLO)))
        k_w0 = tok("s")
        for h in range(8):
            emit("s", S.activation(T.wt[:, 256 * h:256 * h + 256], T.iw[:], COPY, scale=0.0))
        k_wt = tok("s")
        ts(c(GB), d(3), 16.0, A.mult)
        ts(c(AA), d(0), d(1), A.add)
        ts(c(TAU), d(1), 4.0, A.mult, d(4), A.add)
        ts(c(K1), d(5), 4.0, A.is_ge)
        ts(c(MA0), d(2), -1.0, A.mult, 1.0, A.add)
        ts(c(NPAR), d(1), -1.0, A.mult, 1.0, A.add)
        ts(c(C1), d(5), 8.0, A.mult, d(7), A.add)
        ts(c(PP), T.pf[:], 16.0, A.add)
        ts(c(PM), T.pf[:], -16.0, A.add)
        ts(c(ORC), d(6), 2.0, A.mult, 1.0, A.add)

    ds = dests(rank)
    if rank == 0:
        wait("v", (s_r, 64))
        cp("v", T.rb[:], T.rr[:])
        wait("g", tok("v"))
        send([(OWNERS[o], T.rb[:, 32 * o:32 * o + 32], T.druns[:]) for o in ds], even(len(ds), NE), "aruns")
    wait("v", (s_k, 64))
    k_own = None
    if rank < 3:
        cp("v", T.fa[:], T.raw[:, 0:256].indirect(T.lk[:, 0:16]))
        sync("v")
        emit("v", V.transpose(T.fb[:], T.fa[:]))
        sync("v")
        for b in range(2):
            cp("v", T.sl[:, b::2], T.fb[:, 128 * b:128 * b + 128])
        k_sl = tok("v")
        wait("g", k_sl)
        send([(OWNERS[o], T.sl[:, 64 * o:64 * o + 64], T["ls%d" % rank][:]) for o in ds], even(len(ds), NE), "al%d" % rank)
    else:
        for ch in range(2):
            cp("v", T.fa[:, 128 * ch:128 * ch + 128], T.raw[:, ch::2])
        k_tt = tok("v")
        wait("g", k_tt)
        row = 2 * (5 - rank)
        send([(OWNERS[o], T.fa[:, 128 * ch + 32 * o:128 * ch + 32 * o + 32], T.dtop[row + ch]) for o in ds for ch in range(2)],
             even(2 * len(ds), NE), "atop")
        wait("y", k_tt)
        s_o = fresh()
        for ch in range(2):
            dma("y", s_o, T.dtop[row + ch], T.fa[:, 128 * ch + 32 * own:128 * ch + 32 * own + 32])
        k_own = (s_o, 32)
    if rank == 0:
        wait("v", (s_l, 64))
        cp("v", T.lf[:], T.rl[:])
        wait("g", tok("v"))
        send([(OWNERS[o], T.lf[:, 32 * o:32 * o + 32], T.dtop[6]) for o in ds], even(len(ds), NE), "atop")
    wait("v", (s_q, 32))
    for cq in range(4):
        cp("v", T.tf[0:16, 16 * cq:16 * cq + 16], T.tq[0:16, cq::4])
    sync("v")
    emit("v", V.transpose(T.tt[0:32, :], T.tf[0:32, :]))
    sync("v")
    for gb in range(2):
        for a in range(2):
            for w in range(2):
                p0, c0 = 64 * gb + 32 * a, 32 * a + 8 * w + gb
                cp("v", T.xq[p0:p0 + 32, w::2], T.tt[0:32, c0:c0 + 7:2])
    k_xq = tok("v")
    wait("g", k_xq)
    send([(OWNERS[o], T.xq[:, 2 * o:2 * o + 2], T.ql[:, 2 * rank:2 * rank + 2]) for o in ds], even(len(ds), NE), "aq")

    if own is not None:
        def got(r, n):
            return even(n * len(dests(r)), NE)[0]

        s_w0, s_wt = fresh(), fresh()
        total["aruns"] = got(0, 1)
        for q in two:
            wait(q, k_w0, ("aruns", total["aruns"]))
        for rep in range(4):
            dma(two[rep % 2], s_w0, T.w0[16 * rep::64, :], T.druns[:])
        total["atop"] = got(0, 1) + sum(2 * got(r, 2) for r in (3, 4, 5) if r != rank)
        wait("y", k_wt, k_own, ("atop", total["atop"]))
        for G in range(8):
            dma("y", s_wt, T.wt[16 * G:16 * G + 7, :], T.dtop[:, 64 * (G // 4):64 * (G // 4) + 64, :])
        wait("v", k_xq, k_g2)
        ts(c(T0), c(AA), c(GB), A.add)
        ts(c(T1), c(AA), c(GB), A.add, d(1), A.add)
        ts(c(U15), c(TAU), -1.0, A.mult, 15.0, A.add)
        ts(c(CPI), d(6), 16.0, A.mult, c(C1), A.add)
        ts(T.el[:, 8:12], T.iw[:, 0:4], 4.0, A.mult, c(ORC), A.add)
        emit("v", V.memset(T.msk[:], 1.0))
        emit("v", V.memset(T.d5[:, 96:128], 0.0))
        emit("v", V.memset(T.d4[:, 192:256], 0.0))
        emit("v", V.memset(T.ndn[:, 44:48], 0.0))
        sync("v")
        ts(c(LO), c(U15), c(K1), A.mult, c(GB), A.add)
        ts(c(HI1), c(K1), 8.0, A.mult, c(U15), A.add)
        ts(T.el[:, 0:8], T.elf[:, 0:8], c(CPI), A.add)
        emit("v", V.memset(T.msk[:, 0::8], 0.0))
        ma = (c(MA0), d(2))
        for lv, tg in ((0, T0), (1, T1)):
            for a in range(2):
                ts(T.lm[:, 256 * lv + 128 * a:256 * lv + 128 * a + 128], T.rv[:], c(tg), A.is_equal, ma[a], A.mult)
        sync("v")
        ts(c(HI), c(HI1), -8.0, A.add, c(GB), A.add)
        sync("v")
        ts(T.m1[:], T.rv[:], c(LO), A.max, c(HI), A.min)
        for s in range(2):
            for c0 in range(2):
                tg = T.pf[:] if s == c0 else (c(PP) if c0 else c(PM))
                ts(T.sw[:, 256 * s + 128 * c0:256 * s + 128 * c0 + 128], T.iw[:, 0:128], tg, A.is_equal, d(1) if s else c(NPAR), A.mult)
        sync("v")
        tt(T.m2[:], T.m1[:], T.rv[:], A.is_equal)
        sync("v")
        for a in range(2):
            ts(T.lm[:, 512 + 128 * a:640 + 128 * a], T.m2[:], ma[a], A.mult)
        total["aq"] = sum(got(r, 1) for r in range(6) if r != rank)
        wait("v", ("aq", total["aq"]))
        cp("v", T.ql[:, 2 * rank:2 * rank + 2], T.xq[:, 2 * own:2 * own + 2])
        sync("v")
        cp("v", T.l5[:], T.ql[:, 0::2])
        cp("v", T.base[:, 6:12], T.ql[:, 1::2])
        cp("v", T.orep[:], T.ql[:, 0:12].indirect(T.el[:, 8:11]))
        k_c2 = tok("v")
        for q in ("v", "s", "t"):
            wait(q, k_c2)

        wins = [T.w0, T.w1, T.w2, T.w3]
        ready = [(s_w0, 64)]
        st = {}

        def grab(q, name, out, win, lst):
            cp(q, out, win.indirect(lst))
            st[name] = tok(q)

        def turn(out, in_, after):
            wait("v", after)
            emit("v", V.transpose(out, in_))
            sync("v")

        def e5s():
            wait("s", (s_wt, 128))
            grab("s", "g5", T.g5[:], T.wt[:, 0:2048], T.l5[:, 0:6])

        def e5v():
            turn(T.d5[:, 0:96], T.g5[:], st["g5"])
            grab("v", "l4", T.l4[:], T.d5[:, 0:128], T.el[:, 0:1])

        def e4s():
            wait("s", st["l4"])
            grab("s", "g4", T.g4[:], T.wt[:, 0:2048], T.l4[:, 0:12])

        def e4v():
            turn(T.d4[:, 0:192], T.g4[:], st["g4"])
            grab("v", "l3", T.l3[:], T.d4[:, 0:256], T.el[:, 2:4])

        def e3s():
            wait("s", st["l3"])
            grab("s", "g3", T.g3[:], T.wt[:, 0:2048], T.l3[:, 0:24])

        def e3v():
            turn(T.d3[:], T.g3[:], st["g3"])
            grab("v", "nf", T.nf[:], T.d3[:, 0:384], T.el[:, 4:7])
            grab("v", "lq", T.lq[:], T.d3[:, 0:384], T.el[:, 4:7])

        extra = {(1, "s", 0): e5s, (1, "v", 1): e5v, (1, "s", 2): e4s, (2, "v", 0): e4v, (2, "s", 1): e3s, (2, "v", 2): e3v}
        order = [(x, a) for x in (0, 2, 1, 3) for a in range(2)]
        for lv in range(3):
            if lv == rank:
                lst, c0, k_l = T.sl, 64 * own, k_sl
            else:
                total["al%d" % lv] = got(lv, 1)
                lst, c0, k_l = T["ls%d" % lv], 0, ("al%d" % lv, got(lv, 1))
            kg = {}
            for q, xs in (("v", (0, 1)), ("s", (2, 3))):
                wait(q, k_l, *ready)
                for x in xs:
                    cp(q, T.gt[:, 256 * x:256 * x + 256], wins[lv][:, 0:2048].indirect(lst[:, c0 + 16 * x:c0 + 16 * x + 16]))
                    kg[x] = tok(q)
            kp = []
            for b, (x, a) in enumerate(order):
                wait("t", kg[x])
                emit("t", PE.matmul(T["ps%d" % b][:, 0:256], T.lm[:, 256 * lv + 128 * a:256 * lv + 128 * a + 128],
                                    T.gt[:, 256 * x:256 * x + 256], True, True))
                kp.append(tok("t"))
            ready = []
            for i in range(4):
                for q, b in (("s", 2 * i + 1), ("v", 2 * i)):
                    if (lv, q, i) in extra:
                        extra[(lv, q, i)]()
                for q, b in (("v", 2 * i), ("s", 2 * i + 1)):
                    x, a = order[b]
                    wait(q, kp[b])
                    cp(q, wins[lv + 1][:, 1024 * a + 256 * x:1024 * a + 256 * x + 256], T["ps%d" % b][:, 0:256])
                    ready.append(tok(q))
        wait("t", ready[0], st["nf"])
        for s in range(2):
            for c0 in range(2):
                emit("t", PE.matmul(T.ps0[:, 256 + 24 * s:280 + 24 * s], T.sw[:, 256 * s + 128 * c0:256 * s + 128 * c0 + 128],
                                    T.nf[:, c0::2], c0 == 0, c0 == 1))
        k_sw = tok("t")

        for q in ("v", "s"):
            wait(q, st["lq"], *ready)
        grab("v", "qa", T.gq[:, 0:384], T.w3[:, 0:2048], T.lq[:, 0:24])
        grab("s", "qb", T.gq[:, 384:768], T.w3[:, 0:2048], T.lq[:, 24:48])
        wait("s", k_sw)
        for s in range(2):
            cp("s", T.nn[:, s::2], T.ps0[:, 256 + 24 * s:280 + 24 * s])
            cp("s", T.base[:, s:6:2], T.ps0[:, 256 + 24 * s:280 + 24 * s:8])
        k_nn = tok("s")
        wait("v", st["qa"])
        emit("v", V.transpose(T.dq[:, 0:384], T.gq[:, 0:384]))
        wait("v", st["qb"])
        emit("v", V.transpose(T.dq[:, 384:768], T.gq[:, 384:768]))
        sync("v")
        for s in range(2):
            emit("v", V.tensor_tensor_scan(T.cum[:, s::2], T.msk[:, 0:24], T.dq[:, 16 * s::32], 0.0, A.mult, A.add))
        wait("v", k_nn)
        tt(T.ndn[:, 0:46], T.nn[:, 0:46], T.nn[:, 2:48], A.subtract)
        sync("v")
        tt(T.ge[:], T.cum[:], T.orep[:], A.is_le)
        sync("v")
        tt(T.pr[:, 0:48], T.ge[:], T.ndn[:], A.mult)
        tt(T.pr[:, 48:96], T.ge[:], T.dq[:, 0::16], A.mult)
        sync("v")
        for s in range(2):
            emit("v", V.tensor_tensor_scan(T.rs[:, s::2], T.msk[:], T.pr[:, s::2], 0.0, A.mult, A.subtract))
        sync("v")
        for s in range(2):
            tt(T.fin[:, s::2], T.base[:, s::2], T.rs[:, 14 + s::16], A.add)
        sync("v")
        cp("v", T.l2[:], T.fin[:])
        k_l2 = tok("v")
        for q in ("v", "s"):
            wait(q, k_l2)
        grab("v", "ga", T.g2[:, 0:96], T.w3[:, 0:2048], T.l2[:, 0:6])
        grab("s", "gb", T.g2[:, 96:192], T.iw[:, 0:256], T.l2[:, 6:12])
        wait("v", st["ga"])
        turn(T.d2[:], T.g2[:], st["gb"])
        tt(T.hh[:, 0:88], T.d2[:, 0:88], T.d2[:, 96:184], A.is_gt)
        tt(T.nm[:, 0:88], T.d2[:, 0:88], T.d2[:, 96:184], A.is_le)
        sync("v")
        tt(T.hl[:, 0:88], T.hh[:, 0:88], T.d2[:, 8:96], A.mult)
        sync("v")
        emit("v", V.tensor_tensor_scan(T.sel[:, 0:88], T.nm[:, 0:88], T.hl[:, 0:88], 0.0, A.mult, A.add))
        sync("v")
        cp("v", T.l1[:], T.sel[:, 7:88:16])
        sync("v")
        grab("v", "g1", T.g1[:], T.wt[:, 0:2048], T.l1[:, 0:6])
        wait("v", st["g1"])
        emit("v", V.transpose(T.d1[:], T.g1[:]))
        k_d1 = tok("v")
        wait("g", k_d1)
        rs_ = ans_dests(own)
        send([(r, T.d1[:, 16 * r + 6:16 * r + 7], T.dans[own]) for r in rs_], shares(len(rs_), NE), "aans")

    s_y = fresh()
    if own is not None:
        wait("s", k_d1)
        dma("s", s_y, T.y[2 * own:2 * own + 2, :], T.d1[:, 16 * rank + 6:16 * rank + 7])
    total["aans"] = sum(shares(5, NE)[ans_dests(o).index(rank)] for o in range(4) if o != own)
    parts = [(0, 4)] if own is None else [p for p in ((0, own), (own + 1, 4)) if p[0] < p[1]]
    for q, (o0, o1) in zip(two, parts):
        wait(q, ("aans", total["aans"]))
        dma(q, s_y, T.y[2 * o0:2 * o1, :], T.dans[o0:o1])
    wait("g", ("sent", total["sent"]))
    wait("y", (s_y, total[s_y]))
    for name, n in total.items():
        if n and not any(k[1] == name and v >= n for k, v in seen.items()):
            wait("t", (name, n))
